import numpy as np
import ml_dtypes


def mxq(x, axis, fmt="e4m3"):
    dtype, down = {"e4m3": (ml_dtypes.float8_e4m3fn, 7), "e5m2": (ml_dtypes.float8_e5m2, 14)}[fmt]
    v = np.moveaxis(np.asarray(x, np.float32).astype(ml_dtypes.bfloat16).astype(np.float64), axis, -1)
    blocks = v.reshape(v.shape[:-1] + (-1, 32))
    amax = np.abs(blocks).max(-1, keepdims=True)
    byte = np.maximum(np.where(amax > 0, np.frexp(amax)[1] - 1 + 127, 0) - down, 1)
    scale = np.exp2(byte - 127.0)
    codes = (blocks / scale).astype(np.float32).astype(dtype).astype(np.float64)
    return np.moveaxis((codes * scale).reshape(v.shape), -1, axis)


WIDE = False


def mx_kscale(k):
    if not WIDE:
        return np.ones(k)
    levels = np.array([10, -10, 5, -5, 0])
    if k % 512:
        return np.exp2(np.random.permutation(np.resize(levels, k // 32))).repeat(32)
    a = np.empty((k // 512, 16))
    for p in range(k // 512):
        a[p, :8] = np.random.permutation(np.resize(levels, 8))
        for g in range(8):
            far = levels[np.abs(levels - a[p, g]) >= 10]
            a[p, g + 8] = far[np.random.randint(len(far))]
    return np.exp2(a.ravel()).repeat(32)


def f64(x):
    return np.asarray(x).astype(np.float64)


def striped(idx):
    return np.tile(idx.reshape(-1, 16).T, (8, 1)).astype(np.uint16)


def unstriped(offs):
    return offs[:16].T.reshape(-1).astype(np.int64)


E2M1 = np.array([0.0, 0.5, 1.0, 1.5, 2.0, 3.0, 4.0, 6.0, -0.0, -0.5, -1.0, -1.5, -2.0, -3.0, -4.0, -6.0])


def pack_weight(w, fmt):
    k, n = w.shape
    w = f64(np.asarray(w, np.float32).astype(ml_dtypes.bfloat16)).reshape(k // 32, 32, n)
    amax = np.abs(w).max(1)
    if fmt == "e4m3":
        byte = np.frexp(amax)[1] - 1 + 127 - 7
    else:
        mant, ex = np.frexp(amax / 6.0)
        byte = np.where(mant > 0.5, ex, ex - 1) + 127
    byte = np.clip(np.where(amax > 0, byte, 1), 1, 254)
    scaled = (w * np.exp2(127.0 - byte)[:, None, :]).reshape(k, n).astype(np.float32)
    by_word = np.ascontiguousarray(scaled.reshape(k // 512, 128, 4, n).transpose(0, 1, 3, 2))
    if fmt == "e4m3":
        words = by_word.astype(ml_dtypes.float8_e4m3fn).view(np.uint8)
    else:
        c = by_word.astype(ml_dtypes.float4_e2m1fn).view(np.uint8) & 0xF
        words = (c[..., 0::2] | (c[..., 1::2] << 4)).reshape(k // 512, 128, 2 * n)
    return np.ascontiguousarray(words), np.ascontiguousarray(byte.astype(np.uint8).reshape(k // 512, 16, n))


def unpack_weight(words, scales, fmt):
    g, _, n = scales.shape
    words = np.ascontiguousarray(words).reshape(g, 128, n, -1)
    if fmt == "e4m3":
        vals = words.view(ml_dtypes.float8_e4m3fn).astype(np.float64)
    else:
        nib = np.empty((g, 128, n, 4), np.uint8)
        nib[..., 0::2] = words & 0xF
        nib[..., 1::2] = words >> 4
        vals = E2M1[nib]
    vals = vals * np.repeat(np.exp2(scales.astype(np.float64) - 127.0), 8, axis=1)[..., None]
    return vals.transpose(0, 1, 3, 2).reshape(g * 512, n)


def gelu(v):
    return 0.5 * v * (1.0 + np.tanh(np.sqrt(2.0 / np.pi) * (v + 0.044715 * v**3)))


K, T, S, H, T2, P = 1024, 2048, 1024, 512, 2048, 1024

def setup_inputs():
    n = np.random.standard_normal
    s, u = mx_kscale(K)[:, None], mx_kscale(H)[:, None]
    d = {}
    d["tab_words"], d["tab_scales"] = pack_weight(n((K, T)) * s, "e4m3")
    d["w1_words"], d["w1_scales"] = pack_weight(1.7 * n((K, H)) / K ** 0.5 / s, "e2m1")
    d["w2"] = (n((K, H)) / K ** 0.5 / s * u.T).astype(np.float32)
    d["w3_words"], d["w3_scales"] = pack_weight(0.8 * n((K, H)) / K ** 0.5 / s * u.T, "e4m3")
    d["w4"] = (n((H, H)) / H ** 0.5 / u).astype(np.float32)
    d["page0"] = (n((H, T2)) * u).astype(np.float32)
    d["wgs"] = np.exp(0.3 * n((128, S))).astype(np.float32)
    d["near"] = np.exp(0.4 * n(H)).astype(np.float32)
    d["water"] = (np.exp(0.4 * n(H)) / u[:, 0]).astype(np.float32)
    d["offs"] = striped(np.random.permutation(T)[:S])
    d["offs2"] = striped(np.random.permutation(T2)[:S])
    d["offs3"] = striped(np.random.permutation(T2)[:P])
    d["offs4"] = striped(np.random.permutation(T2)[:P])
    return d

def reference(tab_words, tab_scales, w1_words, w1_scales, w2, w3_words, w3_scales, w4,
              page0, wgs, near, water, offs, offs2, offs3, offs4):
    v = unpack_weight(tab_words, tab_scales, "e4m3")[:, unstriped(offs)]
    a = unpack_weight(w1_words, w1_scales, "e2m1").T @ v
    b = mxq(f64(w2), 0, "e4m3").T @ v
    c = unpack_weight(w3_words, w3_scales, "e4m3").T @ v
    h = np.tanh(a) * np.abs(b) + c
    page = f64(page0).copy()
    page[:, unstriped(offs2)] = np.tile(f64(wgs), (H // 128, 1)) * h
    x = f64(near)[:, None] * page[:, unstriped(offs3)]
    y = mxq(f64(w4), 0, "e4m3").T @ mxq(x, 0, "e4m3")
    hole = f64(water)[:, None] * page[:, unstriped(offs4)]
    return np.maximum(y, hole) + y

@@ -1,0 +1,296 @@
+from contextlib import ExitStack
+
+import concourse.mybir as mybir
+from concourse.masks import make_identity
+
+K, T, S, H, T2, M = 1024, 2048, 1024, 512, 2048, 1024
+FLOPS = 2 * K * H * S * 3 + 2 * H * H * M
+
+F32 = mybir.dt.float32
+BF16 = mybir.dt.bfloat16
+I32 = mybir.dt.int32
+U32 = mybir.dt.uint32
+U16 = mybir.dt.uint16
+U8 = mybir.dt.uint8
+FP8X4 = mybir.dt.float8_e4m3fn_x4
+FP4X4 = mybir.dt.float4_e2m1fn_x4
+ALU = mybir.AluOpType
+ACT = mybir.ActivationFunctionType
+
+P = 128
+PACK = 4
+PASSES = K // (P * PACK)
+TILES = H // P
+HALF = 512
+CH = HALF // P
+PIECES = ((0, 256), (256, 512), (512, 768), (768, 1024))
+
+
+def tile_list_tremor_corridor_board_kernel(
+    tc, tab_words, tab_scales, w1_words, w1_scales, w2, w3_words, w3_scales, w4,
+    page0, wgs, near, water, offs, offs2, offs3, offs4, out,
+):
+    nc = tc.nc
+    with ExitStack() as ctx:
+        keep = ctx.enter_context(tc.tile_pool(name="keep", bufs=1))
+        work = ctx.enter_context(tc.tile_pool(name="work", bufs=2))
+        psum = ctx.enter_context(tc.psum_pool(name="psum", bufs=1))
+
+        list1 = keep.tile([P, S // 16], U16, name="list1")
+        list2 = keep.tile([P, S // 16], U16, name="list2")
+        list3 = keep.tile([P, M // 16], U16, name="list3")
+        list4 = keep.tile([P, M // 16], U16, name="list4")
+        tab_s = keep.tile([P, T], U8, name="tab_s", align_bytes=64)
+        w1_s = keep.tile([P, PASSES, H], U8, name="w1_s", align_bytes=64)
+        w3_s = keep.tile([P, PASSES, H], U8, name="w3_s", align_bytes=64)
+        v_s_low = keep.tile([P, S], U8, name="v_s_low", align_bytes=64)
+        nc.vector.memset(tab_s[:].bitcast(I32), 0)
+        nc.vector.memset(w1_s[:].bitcast(I32), 0)
+        nc.vector.memset(v_s_low[:].bitcast(I32), 0)
+        nc.gpsimd.memset(w3_s[:].bitcast(I32), 0)
+
+        def load_plane(queue, plane, src):
+            for q in range(4):
+                queue.dma_start(
+                    plane[32 * q : 32 * q + 4, :, :].bitcast(I32),
+                    src[:, 4 * q : 4 * q + 4, :].rearrange("a r n -> r a n").bitcast(I32),
+                )
+
+        w2_rows = w2.rearrange("(a p i) c -> a p i c", a=PASSES, i=PACK)
+
+        def load_w2(c0, c1):
+            tiles = []
+            for a in range(PASSES):
+                raw = keep.tile([P, PACK, c1 - c0], F32, name="w2_raw%d_%d" % (a, c0))
+                nc.sync.dma_start(raw[:], w2_rows[a, :, :, c0:c1])
+                tiles.append(raw)
+            return [[raw[:, :, c : c + P] for raw in tiles] for c in range(0, c1 - c0, P)]
+
+        page = [keep.tile([P, T2], F32, name="page%d" % t) for t in range(TILES)]
+        wgs_sb = [keep.tile([P, HALF], F32, name="wgs_sb%d" % hf) for hf in range(2)]
+        w3_w = keep.tile([P, PASSES, H], I32, name="w3_w", align_bytes=64)
+        w1_w = keep.tile([P, PASSES, 2 * H], U8, name="w1_w", align_bytes=64)
+        near_sb = keep.tile([P, TILES], F32, name="near_sb")
+        water_sb = keep.tile([P, TILES], F32, name="water_sb")
+        w4_raw = keep.tile([P, PACK, H], F32, name="w4_raw")
+        tab_w = keep.tile([P, PASSES, T], I32, name="tab_w", align_bytes=64)
+        tab_rows = tab_words.rearrange("a p t i -> p a (t i)").bitcast(I32)
+        w2_raw = []
+        nc.sync.dma_start(list1[:], offs)
+        for q in range(4):
+            nc.scalar.dma_start(tab_s[32 * q : 32 * q + 8, :].bitcast(I32), tab_scales[:, 4 * q : 4 * q + 4, :].bitcast(I32))
+        load_plane(nc.scalar, w1_s, w1_scales)
+        load_plane(nc.gpsimd, w3_s, w3_scales)
+        nc.sync.dma_start(tab_w[:, 0, :], tab_rows[:, 0, :])
+        nc.sync.dma_start(tab_w[:, 1, :], tab_rows[:, 1, :])
+        w2_raw = w2_raw + load_w2(0, 2 * P)
+        nc.sync.dma_start(w1_w[:].bitcast(I32), w1_words.rearrange("a p n -> p a n").bitcast(I32))
+        nc.sync.dma_start(w3_w[:], w3_words.rearrange("a p c i -> p a (c i)").bitcast(I32))
+        nc.sync.dma_start(list2[:], offs2)
+        nc.sync.dma_start(wgs_sb[0][:], wgs[:, 0:HALF])
+        nc.sync.dma_start(page[0][:], page0[0:P, :])
+        nc.sync.dma_start(wgs_sb[1][:], wgs[:, HALF:S])
+        w2_raw = w2_raw + load_w2(2 * P, H)
+        nc.sync.dma_start(page[1][:], page0[P : 2 * P, :])
+        nc.sync.dma_start(page[2][:], page0[2 * P : 3 * P, :])
+        nc.sync.dma_start(list3[:], offs3)
+        with nc.allow_non_contiguous_dma(reason="one factor a partition"):
+            nc.sync.dma_start(near_sb[:], near.rearrange("(t p) -> p t", p=P))
+            nc.sync.dma_start(water_sb[:], water.rearrange("(t p) -> p t", p=P))
+        nc.sync.dma_start(w4_raw[:], w4.rearrange("(p i) c -> p i c", i=PACK))
+        nc.sync.dma_start(page[3][:], page0[3 * P : 4 * P, :])
+        nc.sync.dma_start(list4[:], offs4)
+
+        ident_f = keep.tile([P, P], F32, name="ident_f")
+        ident_b = keep.tile([P, P], BF16, name="ident_b")
+        make_identity(nc, ident_f[:])
+        make_identity(nc, ident_b[:])
+        warm = keep.tile([P, 1], F32, name="warm")
+        nc.scalar.activation(warm[:], ident_f[:, 0:1], ACT.Tanh)
+
+        v_w = {}
+        v_s = keep.tile([P, S], U8, name="v_s", align_bytes=64)
+        nc.vector.tensor_copy(v_s[:], tab_s[:].indirect(list1[:]))
+        for q in range(4):
+            nc.scalar.dma_start(v_s_low[32 * q : 32 * q + 4, :].bitcast(I32), v_s[32 * q + 4 : 32 * q + 8, :].bitcast(I32))
+
+        def gather_words(n, tag):
+            j0, j1 = PIECES[n]
+            g = keep.tile([P, PASSES, j1 - j0], U32, name="v_w", tag=tag, align_bytes=64)
+            for a in range(PASSES):
+                nc.vector.tensor_copy(g[:, a, :], tab_w[:, a, :].bitcast(U32).indirect(list1[:, j0 // 16 : j1 // 16]))
+                for c in range((j1 - j0) // P):
+                    v_w[a, j0 // P + c] = g[:, a, c * P : (c + 1) * P]
+
+
+        def interleave(dst, src):
+            nc.scalar.copy(
+                dst.rearrange("p (c f) i -> p c i f", f=4), src.rearrange("p i (c f) -> p c i f", f=4)
+            )
+
+        w2_w, w2_s = [], []
+
+        def quantise_w2(t, tag):
+            grouped = keep.tile([P, PASSES, P, PACK], BF16, name="w2_grouped", tag=tag, align_bytes=64)
+            for a in range(PASSES):
+                interleave(grouped[:, a, :, :], w2_raw[t][a])
+            codes = keep.tile([P, PASSES, P], U32, name="w2_w%d" % t, align_bytes=64)
+            scales = keep.tile([P, PASSES, P], U8, name="w2_s%d" % t, align_bytes=64)
+            nc.vector.quantize_mx(
+                out=codes[:].rearrange("p a c -> p (a c)").bitcast(FP8X4),
+                scales=scales[:].rearrange("p a c -> p (a c)"),
+                in_=grouped[:].rearrange("p a c i -> p (a c i)"),
+            )
+            w2_w.append(codes)
+            w2_s.append(scales)
+
+        units = [(0, j0, j1) for j0, j1 in PIECES]
+        units = units + [(t, j0, j0 + HALF) for t in range(1, TILES) for j0 in (0, HALF)]
+
+        def first_stage(unit):
+            t, j0, j1 = units[unit]
+            chunks = (j1 - j0) // P
+            rows = slice(t * P, (t + 1) * P)
+            sums = []
+            for name, tag in (("a", "bank_a"), ("b", "bank_b%d" % (unit % 2)), ("c", "bank_c")):
+                bank = psum.tile([P, chunks, P], F32, name="bank_" + name, tag=tag)
+                for c in range(chunks):
+                    for a in range(PASSES):
+                        cols = slice(j0 + c * P, j0 + (c + 1) * P)
+                        lhs_s = v_s[4 * a : P, cols]
+                        if name == "a":
+                            lhs_s = (v_s, v_s_low)[a][:, cols]
+                            rhs = w1_w[:, a, 2 * t * P : 2 * (t + 1) * P].bitcast(FP4X4)
+                            rhs_s = w1_s[:, a, rows]
+                        elif name == "b":
+                            rhs = w2_w[t][:, a, :].bitcast(FP8X4)
+                            rhs_s = w2_s[t][:, a, :]
+                        else:
+                            rhs = w3_w[:, a, rows].bitcast(FP8X4)
+                            rhs_s = w3_s[:, a, rows]
+                        nc.tensor.matmul_mx(
+                            bank[:, c, :],
+                            lhsT=v_w[a, j0 // P + c].bitcast(FP8X4), lhsT_scale=lhs_s,
+                            rhs=rhs, rhs_scale=rhs_s, start=(a == 0), stop=(a == PASSES - 1),
+                        )
+                sums.append(bank)
+            strength = work.tile([P, chunks, P], F32, name="strength")
+            if unit == 0:
+                direction = keep.tile([P, chunks, P], F32, name="direction", tag="after_first_product", align_bytes=64)
+            else:
+                direction = work.tile([P, chunks, P], F32, name="direction")
+            plain = work.tile([P, chunks, P], F32, name="plain")
+            nc.scalar.activation(direction[:], sums[0][:], ACT.Tanh)
+            nc.scalar.activation(strength[:], sums[1][:], ACT.Abs)
+            nc.scalar.copy(plain[:], sums[2][:])
+            product = keep.tile([P, chunks, P], F32, name="product", tag="product%d" % unit, align_bytes=64)
+            nc.vector.tensor_tensor(product[:], direction[:], strength[:], ALU.mult)
+            return plain, product
+
+        def turn_and_put(unit, plain, product):
+            t, j0, j1 = units[unit]
+            chunks = (j1 - j0) // P
+            bank_h = psum.tile([P, chunks, P], F32, name="bank_h", tag="bank_b%d" % ((unit + 1) % 2))
+            for c in range(chunks):
+                nc.tensor.matmul(bank_h[:, c, :], lhsT=plain[:, c, :], rhs=ident_f[:], is_transpose=True, start=True, stop=False)
+                nc.tensor.matmul(bank_h[:, c, :], lhsT=product[:, c, :], rhs=ident_f[:], is_transpose=True, start=False, stop=True)
+            if unit == len(units) - 1:
+                h = keep.tile([P, j1 - j0], F32, name="h_last", tag="late")
+            else:
+                h = work.tile([P, j1 - j0], F32, name="h")
+            nc.scalar.copy(h[:], bank_h[:].rearrange("p c j -> p (c j)"))
+            nc.vector.tensor_tensor(page[t][:].indirect(list2[:, j0 // 16 : j1 // 16]), h[:], wgs_sb[j0 // HALF][:, j0 % HALF : j0 % HALF + j1 - j0], ALU.mult)
+
+        x_turned = [keep.tile([P, CH, 2, P], F32, name="x_turned%d" % hf) for hf in range(2)]
+
+        def reread(t, hf):
+            x_rows = work.tile([P, HALF], BF16, name="x_rows")
+            nc.scalar.activation(x_rows[:], picked[:, hf, t, :], ACT.Copy, scale=near_sb[:, t : t + 1])
+            bank_t = psum.tile([P, CH, P], BF16, name="bank_t", tag="bank_t", bufs=2)
+            for c in range(CH):
+                nc.tensor.transpose(bank_t[:, c, :], x_rows[:, c * P : (c + 1) * P], ident_b[:])
+            nc.scalar.copy(
+                x_turned[hf][:, :, :, 32 * t : 32 * (t + 1)],
+                bank_t[:].bitcast(F32).rearrange("m c (q u) -> m c u q", u=2),
+            )
+
+        w4_w = keep.tile([P, H], U32, name="w4_w", align_bytes=64)
+        w4_s = keep.tile([P, H], U8, name="w4_s", align_bytes=64)
+
+        def quantise_w4(tag):
+            grouped = keep.tile([P, H, PACK], BF16, name="w4_grouped", tag=tag, align_bytes=64)
+            interleave(grouped[:], w4_raw[:])
+            nc.vector.quantize_mx(out=w4_w[:].bitcast(FP8X4), scales=w4_s[:], in_=grouped[:].rearrange("p c i -> p (c i)"))
+
+        quantise_w2(0, "w2_first")
+        quantise_w2(1, "w2_second")
+        for n in range(len(PIECES) - 1):
+            gather_words(n, "v_w%d" % n)
+        ahead = first_stage(0)
+        gather_words(len(PIECES) - 1, "after_first_product")
+        for unit in range(len(units)):
+            parts = ahead
+            if unit + 1 < len(units):
+                ahead = first_stage(unit + 1)
+            turn_and_put(unit, *parts)
+            if unit in (1, 3, 99):
+                quantise_w2(len(w2_w), "product%d" % unit)
+            if unit == 6:
+                quantise_w4("product%d" % unit)
+
+        picked = keep.tile([P, 3, TILES, HALF], F32, name="picked", tag="late")
+        for hf in range(2):
+            for t in range(TILES):
+                nc.vector.tensor_copy(picked[:, hf, t, :], page[t][:].indirect(list3[:, hf * 32 : (hf + 1) * 32]))
+        holes = [picked[:, 2, :, :]]
+        for t in range(TILES):
+            nc.vector.tensor_copy(holes[0][:, t, :], page[t][:].indirect(list4[:, 0:32]))
+        for hf in range(2):
+            for t in range(TILES):
+                reread(t, hf)
+
+        x_w, x_s = [], []
+        for hf in range(2):
+            grouped = keep.tile([P, HALF, PACK], BF16, name="x_grouped", tag="x_grouped%d" % hf, align_bytes=64)
+            words = grouped[:].bitcast(F32)
+            for pair in range(CH // 2):
+                bank_x = psum.tile([P, 2, 2, P], F32, name="bank_x", tag="bank_x", bufs=2)
+                for c in range(2):
+                    for u in range(2):
+                        nc.tensor.transpose(bank_x[:, c, u, :], x_turned[hf][:, 2 * pair + c, u, :], ident_f[:])
+                nc.scalar.copy(
+                    words[:, pair * 2 * P : (pair + 1) * 2 * P, :].rearrange("p (c m) u -> p c m u", c=2),
+                    bank_x[:].rearrange("p c u m -> p c m u"),
+                )
+            codes = keep.tile([P, HALF], U32, name="x_w%d" % hf, align_bytes=64)
+            scales = keep.tile([P, HALF], U8, name="x_s%d" % hf, align_bytes=64)
+            nc.vector.quantize_mx(out=codes[:].bitcast(FP8X4), scales=scales[:], in_=grouped[:].rearrange("p m i -> p (m i)"))
+            x_w.append(codes)
+            x_s.append(scales)
+            if hf == 0:
+                second = keep.tile([P, TILES, HALF], F32, name="holes", tag="x_grouped0", align_bytes=64)
+                for t in range(TILES):
+                    nc.vector.tensor_copy(second[:, t, :], page[t][:].indirect(list4[:, 32:64]))
+                holes.append(second[:])
+
+        tags = ("bank_a", "bank_b0", "bank_b1", "bank_c")
+        pending = None
+
+        def finish(hf, t, y, larger):
+            result = picked[:, hf, t, :]
+            nc.vector.tensor_tensor(result, larger[:], y[:], ALU.add)
+            nc.sync.dma_start(out[t * P : (t + 1) * P, hf * HALF : (hf + 1) * HALF], result)
+
+        for hf in range(2):
+            for t in range(TILES):
+                y = psum.tile([P, HALF], F32, name="y", tag=tags[t])
+                nc.tensor.matmul_mx(
+                    y[:], lhsT=w4_w[:, t * P : (t + 1) * P].bitcast(FP8X4), lhsT_scale=w4_s[:, t * P : (t + 1) * P],
+                    rhs=x_w[hf][:].bitcast(FP8X4), rhs_scale=x_s[hf][:], start=True, stop=True,
+                )
+                larger = work.tile([P, HALF], F32, name="larger", bufs=3)
+                nc.vector.scalar_tensor_tensor(larger[:], holes[hf][:, t, :], water_sb[:, t : t + 1], y[:], ALU.mult, ALU.max)
+                if pending is not None:
+                    finish(*pending)
+                pending = (hf, t, y, larger)
+        finish(*pending)

@@ -242,15 +242,21 @@ def tile_list_tremor_corridor_board_kernel(
         for hf in range(2):
             for t in range(TILES):
                 nc.vector.tensor_copy(picked[:, hf, t, :], page[t][:].indirect(list3[:, hf * 32 : (hf + 1) * 32]))
-        holes = [picked[:, 2, :, :]]
-        for t in range(TILES):
-            nc.vector.tensor_copy(holes[0][:, t, :], page[t][:].indirect(list4[:, 0:32]))
-        for hf in range(2):
-            for t in range(TILES):
-                reread(t, hf)
+        finals = [(hf, t) for hf in range(2) for t in range(TILES)]
+        holes = {}
+
+        def gather_holes(n, dst):
+            hf, t = finals[n]
+            nc.vector.tensor_copy(dst, page[t][:].indirect(list4[:, hf * 32 : (hf + 1) * 32]))
+            holes[n] = dst
+
+        for n in range(3):
+            gather_holes(n, picked[:, 2, n, :])
 
         x_w, x_s = [], []
         for hf in range(2):
+            for t in range(TILES):
+                reread(t, hf)
             grouped = keep.tile([P, HALF, PACK], BF16, name="x_grouped", tag="x_grouped%d" % hf, align_bytes=64)
             words = grouped[:].bitcast(F32)
             for pair in range(CH // 2):
@@ -268,29 +274,37 @@ def tile_list_tremor_corridor_board_kernel(
             x_w.append(codes)
             x_s.append(scales)
             if hf == 0:
-                second = keep.tile([P, TILES, HALF], F32, name="holes", tag="x_grouped0", align_bytes=64)
-                for t in range(TILES):
-                    nc.vector.tensor_copy(second[:, t, :], page[t][:].indirect(list4[:, 32:64]))
-                holes.append(second[:])
+                held = keep.tile([P, 5 - 3, HALF], F32, name="held", tag="x_grouped0", align_bytes=64)
+                for n in range(3, 5):
+                    gather_holes(n, held[:, n - 3, :])
 
         tags = ("bank_a", "bank_b0", "bank_b1", "bank_c")
-        pending = None
-
-        def finish(hf, t, y, larger):
-            result = picked[:, hf, t, :]
-            nc.vector.tensor_tensor(result, larger[:], y[:], ALU.add)
-            nc.sync.dma_start(out[t * P : (t + 1) * P, hf * HALF : (hf + 1) * HALF], result)
-
-        for hf in range(2):
-            for t in range(TILES):
+        waiting = []
+        for n, (hf, t) in enumerate(finals):
+            if hf == 0:
+                y = psum.tile([P, HALF], F32, name="y", tag="bank_x", bufs=2)
+            else:
                 y = psum.tile([P, HALF], F32, name="y", tag=tags[t])
-                nc.tensor.matmul_mx(
-                    y[:], lhsT=w4_w[:, t * P : (t + 1) * P].bitcast(FP8X4), lhsT_scale=w4_s[:, t * P : (t + 1) * P],
-                    rhs=x_w[hf][:].bitcast(FP8X4), rhs_scale=x_s[hf][:], start=True, stop=True,
-                )
-                larger = work.tile([P, HALF], F32, name="larger", bufs=3)
-                nc.vector.scalar_tensor_tensor(larger[:], holes[hf][:, t, :], water_sb[:, t : t + 1], y[:], ALU.mult, ALU.max)
-                if pending is not None:
-                    finish(*pending)
-                pending = (hf, t, y, larger)
-        finish(*pending)
+            nc.tensor.matmul_mx(
+                y[:], lhsT=w4_w[:, t * P : (t + 1) * P].bitcast(FP8X4), lhsT_scale=w4_s[:, t * P : (t + 1) * P],
+                rhs=x_w[hf][:].bitcast(FP8X4), rhs_scale=x_s[hf][:], start=True, stop=True,
+            )
+            larger = work.tile([P, HALF], F32, name="larger", bufs=4)
+            result = picked[:, hf, t, :]
+            rows = out[t * P : (t + 1) * P, hf * HALF : (hf + 1) * HALF]
+            if n < 6:
+                y_sb = work.tile([P, HALF], F32, name="y_sb", bufs=4)
+                nc.scalar.copy(y_sb[:], y[:])
+            nc.vector.scalar_tensor_tensor(larger[:], holes[n], water_sb[:, t : t + 1], y[:], ALU.mult, ALU.max)
+            if n + 5 < len(finals):
+                gather_holes(n + 5, holes[n])
+            if n < 6:
+                nc.gpsimd.tensor_tensor(result, larger[:], y_sb[:], ALU.add)
+                nc.sync.dma_start(rows, result)
+            else:
+                waiting.append((result, larger, y, rows))
+            if len(waiting) == 2 or n == len(finals) - 1:
+                for result, larger, y, rows in waiting[: (1 if n < len(finals) - 1 else 2)]:
+                    nc.vector.tensor_tensor(result, larger[:], y[:], ALU.add)
+                    nc.sync.dma_start(rows, result)
+                waiting = waiting[1:]

from contextlib import ExitStack

import concourse.mybir as mybir
from concourse.masks import make_identity

K, T, S, H, T2, M = 1024, 2048, 1024, 512, 2048, 1024
FLOPS = 2 * K * H * S * 3 + 2 * H * H * M

F32 = mybir.dt.float32
BF16 = mybir.dt.bfloat16
I32 = mybir.dt.int32
U32 = mybir.dt.uint32
U16 = mybir.dt.uint16
U8 = mybir.dt.uint8
FP8X4 = mybir.dt.float8_e4m3fn_x4
FP4X4 = mybir.dt.float4_e2m1fn_x4
ALU = mybir.AluOpType
ACT = mybir.ActivationFunctionType

P = 128
PACK = 4
PASSES = K // (P * PACK)
TILES = H // P
HALF = 512
CH = HALF // P
PIECES = ((0, 256), (256, 512), (512, 768), (768, 1024))


def tile_list_tremor_corridor_board_kernel(
    tc, tab_words, tab_scales, w1_words, w1_scales, w2, w3_words, w3_scales, w4,
    page0, wgs, near, water, offs, offs2, offs3, offs4, out,
):
    nc = tc.nc
    with ExitStack() as ctx:
        keep = ctx.enter_context(tc.tile_pool(name="keep", bufs=1))
        work = ctx.enter_context(tc.tile_pool(name="work", bufs=2))
        psum = ctx.enter_context(tc.psum_pool(name="psum", bufs=1))

        list1 = keep.tile([P, S // 16], U16, name="list1")
        list2 = keep.tile([P, S // 16], U16, name="list2")
        list3 = keep.tile([P, M // 16], U16, name="list3")
        list4 = keep.tile([P, M // 16], U16, name="list4")
        tab_s = keep.tile([P, T], U8, name="tab_s", align_bytes=64)
        w1_s = keep.tile([P, PASSES, H], U8, name="w1_s", align_bytes=64)
        w3_s = keep.tile([P, PASSES, H], U8, name="w3_s", align_bytes=64)
        v_s_low = keep.tile([P, S], U8, name="v_s_low", align_bytes=64)
        nc.vector.memset(tab_s[:].bitcast(I32), 0)
        nc.vector.memset(w1_s[:].bitcast(I32), 0)
        nc.vector.memset(v_s_low[:].bitcast(I32), 0)
        nc.gpsimd.memset(w3_s[:].bitcast(I32), 0)

        def load_plane(queue, plane, src):
            for q in range(4):
                queue.dma_start(
                    plane[32 * q : 32 * q + 4, :, :].bitcast(I32),
                    src[:, 4 * q : 4 * q + 4, :].rearrange("a r n -> r a n").bitcast(I32),
                )

        w2_rows = w2.rearrange("(a p i) c -> a p i c", a=PASSES, i=PACK)

        def load_w2(c0, c1):
            tiles = []
            for a in range(PASSES):
                raw = keep.tile([P, PACK, c1 - c0], F32, name="w2_raw%d_%d" % (a, c0))
                nc.sync.dma_start(raw[:], w2_rows[a, :, :, c0:c1])
                tiles.append(raw)
            return [[raw[:, :, c : c + P] for raw in tiles] for c in range(0, c1 - c0, P)]

        page = [keep.tile([P, T2], F32, name="page%d" % t) for t in range(TILES)]
        wgs_sb = [keep.tile([P, HALF], F32, name="wgs_sb%d" % hf) for hf in range(2)]
        w3_w = keep.tile([P, PASSES, H], I32, name="w3_w", align_bytes=64)
        w1_w = keep.tile([P, PASSES, 2 * H], U8, name="w1_w", align_bytes=64)
        near_sb = keep.tile([P, TILES], F32, name="near_sb")
        water_sb = keep.tile([P, TILES], F32, name="water_sb")
        w4_raw = keep.tile([P, PACK, H], F32, name="w4_raw")
        tab_w = keep.tile([P, PASSES, T], I32, name="tab_w", align_bytes=64)
        tab_rows = tab_words.rearrange("a p t i -> p a (t i)").bitcast(I32)
        w2_raw = []
        nc.sync.dma_start(list1[:], offs)
        for q in range(4):
            nc.scalar.dma_start(tab_s[32 * q : 32 * q + 8, :].bitcast(I32), tab_scales[:, 4 * q : 4 * q + 4, :].bitcast(I32))
        load_plane(nc.scalar, w1_s, w1_scales)
        load_plane(nc.gpsimd, w3_s, w3_scales)
        nc.sync.dma_start(tab_w[:, 0, :], tab_rows[:, 0, :])
        nc.sync.dma_start(tab_w[:, 1, :], tab_rows[:, 1, :])
        w2_raw = w2_raw + load_w2(0, 2 * P)
        nc.sync.dma_start(w1_w[:].bitcast(I32), w1_words.rearrange("a p n -> p a n").bitcast(I32))
        nc.sync.dma_start(w3_w[:], w3_words.rearrange("a p c i -> p a (c i)").bitcast(I32))
        nc.sync.dma_start(list2[:], offs2)
        nc.sync.dma_start(wgs_sb[0][:], wgs[:, 0:HALF])
        nc.sync.dma_start(page[0][:], page0[0:P, :])
        nc.sync.dma_start(wgs_sb[1][:], wgs[:, HALF:S])
        w2_raw = w2_raw + load_w2(2 * P, H)
        nc.sync.dma_start(page[1][:], page0[P : 2 * P, :])
        nc.sync.dma_start(page[2][:], page0[2 * P : 3 * P, :])
        nc.sync.dma_start(list3[:], offs3)
        with nc.allow_non_contiguous_dma(reason="one factor a partition"):
            nc.sync.dma_start(near_sb[:], near.rearrange("(t p) -> p t", p=P))
            nc.sync.dma_start(water_sb[:], water.rearrange("(t p) -> p t", p=P))
        nc.sync.dma_start(w4_raw[:], w4.rearrange("(p i) c -> p i c", i=PACK))
        nc.sync.dma_start(page[3][:], page0[3 * P : 4 * P, :])
        nc.sync.dma_start(list4[:], offs4)

        ident_f = keep.tile([P, P], F32, name="ident_f")
        ident_b = keep.tile([P, P], BF16, name="ident_b")
        make_identity(nc, ident_f[:])
        make_identity(nc, ident_b[:])
        warm = keep.tile([P, 1], F32, name="warm")
        nc.scalar.activation(warm[:], ident_f[:, 0:1], ACT.Tanh)

        v_w = {}
        v_s = keep.tile([P, S], U8, name="v_s", align_bytes=64)
        nc.vector.tensor_copy(v_s[:], tab_s[:].indirect(list1[:]))
        for q in range(4):
            nc.scalar.dma_start(v_s_low[32 * q : 32 * q + 4, :].bitcast(I32), v_s[32 * q + 4 : 32 * q + 8, :].bitcast(I32))

        def gather_words(n, tag):
            j0, j1 = PIECES[n]
            g = keep.tile([P, PASSES, j1 - j0], U32, name="v_w", tag=tag, align_bytes=64)
            for a in range(PASSES):
                nc.vector.tensor_copy(g[:, a, :], tab_w[:, a, :].bitcast(U32).indirect(list1[:, j0 // 16 : j1 // 16]))
                for c in range((j1 - j0) // P):
                    v_w[a, j0 // P + c] = g[:, a, c * P : (c + 1) * P]


        def interleave(dst, src):
            nc.scalar.copy(
                dst.rearrange("p (c f) i -> p c i f", f=4), src.rearrange("p i (c f) -> p c i f", f=4)
            )

        w2_w, w2_s = [], []

        def quantise_w2(t, tag):
            grouped = keep.tile([P, PASSES, P, PACK], BF16, name="w2_grouped", tag=tag, align_bytes=64)
            for a in range(PASSES):
                interleave(grouped[:, a, :, :], w2_raw[t][a])
            codes = keep.tile([P, PASSES, P], U32, name="w2_w%d" % t, align_bytes=64)
            scales = keep.tile([P, PASSES, P], U8, name="w2_s%d" % t, align_bytes=64)
            nc.vector.quantize_mx(
                out=codes[:].rearrange("p a c -> p (a c)").bitcast(FP8X4),
                scales=scales[:].rearrange("p a c -> p (a c)"),
                in_=grouped[:].rearrange("p a c i -> p (a c i)"),
            )
            w2_w.append(codes)
            w2_s.append(scales)

        units = [(0, j0, j1) for j0, j1 in PIECES]
        units = units + [(t, j0, j0 + HALF) for t in range(1, TILES) for j0 in (0, HALF)]

        def first_stage(unit):
            t, j0, j1 = units[unit]
            chunks = (j1 - j0) // P
            rows = slice(t * P, (t + 1) * P)
            sums = []
            for name, tag in (("a", "bank_a"), ("b", "bank_b%d" % (unit % 2)), ("c", "bank_c")):
                bank = psum.tile([P, chunks, P], F32, name="bank_" + name, tag=tag)
                for c in range(chunks):
                    for a in range(PASSES):
                        cols = slice(j0 + c * P, j0 + (c + 1) * P)
                        lhs_s = v_s[4 * a : P, cols]
                        if name == "a":
                            lhs_s = (v_s, v_s_low)[a][:, cols]
                            rhs = w1_w[:, a, 2 * t * P : 2 * (t + 1) * P].bitcast(FP4X4)
                            rhs_s = w1_s[:, a, rows]
                        elif name == "b":
                            rhs = w2_w[t][:, a, :].bitcast(FP8X4)
                            rhs_s = w2_s[t][:, a, :]
                        else:
                            rhs = w3_w[:, a, rows].bitcast(FP8X4)
                            rhs_s = w3_s[:, a, rows]
                        nc.tensor.matmul_mx(
                            bank[:, c, :],
                            lhsT=v_w[a, j0 // P + c].bitcast(FP8X4), lhsT_scale=lhs_s,
                            rhs=rhs, rhs_scale=rhs_s, start=(a == 0), stop=(a == PASSES - 1),
                        )
                sums.append(bank)
            strength = work.tile([P, chunks, P], F32, name="strength")
            if unit == 0:
                direction = keep.tile([P, chunks, P], F32, name="direction", tag="after_first_product", align_bytes=64)
            else:
                direction = work.tile([P, chunks, P], F32, name="direction")
            plain = work.tile([P, chunks, P], F32, name="plain")
            nc.scalar.activation(direction[:], sums[0][:], ACT.Tanh)
            nc.scalar.activation(strength[:], sums[1][:], ACT.Abs)
            nc.scalar.copy(plain[:], sums[2][:])
            product = keep.tile([P, chunks, P], F32, name="product", tag="product%d" % unit, align_bytes=64)
            nc.vector.tensor_tensor(product[:], direction[:], strength[:], ALU.mult)
            return plain, product

        def turn_and_put(unit, plain, product):
            t, j0, j1 = units[unit]
            chunks = (j1 - j0) // P
            bank_h = psum.tile([P, chunks, P], F32, name="bank_h", tag="bank_b%d" % ((unit + 1) % 2))
            for c in range(chunks):
                nc.tensor.matmul(bank_h[:, c, :], lhsT=plain[:, c, :], rhs=ident_f[:], is_transpose=True, start=True, stop=False)
                nc.tensor.matmul(bank_h[:, c, :], lhsT=product[:, c, :], rhs=ident_f[:], is_transpose=True, start=False, stop=True)
            if unit == len(units) - 1:
                h = keep.tile([P, j1 - j0], F32, name="h_last", tag="late")
            else:
                h = work.tile([P, j1 - j0], F32, name="h")
            nc.scalar.copy(h[:], bank_h[:].rearrange("p c j -> p (c j)"))
            nc.vector.tensor_tensor(page[t][:].indirect(list2[:, j0 // 16 : j1 // 16]), h[:], wgs_sb[j0 // HALF][:, j0 % HALF : j0 % HALF + j1 - j0], ALU.mult)

        x_turned = [keep.tile([P, CH, 2, P], F32, name="x_turned%d" % hf) for hf in range(2)]

        def reread(t, hf):
            x_rows = work.tile([P, HALF], BF16, name="x_rows")
            nc.scalar.activation(x_rows[:], picked[:, hf, t, :], ACT.Copy, scale=near_sb[:, t : t + 1])
            bank_t = psum.tile([P, CH, P], BF16, name="bank_t", tag="bank_t", bufs=2)
            for c in range(CH):
                nc.tensor.transpose(bank_t[:, c, :], x_rows[:, c * P : (c + 1) * P], ident_b[:])
            nc.scalar.copy(
                x_turned[hf][:, :, :, 32 * t : 32 * (t + 1)],
                bank_t[:].bitcast(F32).rearrange("m c (q u) -> m c u q", u=2),
            )

        w4_w = keep.tile([P, H], U32, name="w4_w", align_bytes=64)
        w4_s = keep.tile([P, H], U8, name="w4_s", align_bytes=64)

        def quantise_w4(tag):
            grouped = keep.tile([P, H, PACK], BF16, name="w4_grouped", tag=tag, align_bytes=64)
            interleave(grouped[:], w4_raw[:])
            nc.vector.quantize_mx(out=w4_w[:].bitcast(FP8X4), scales=w4_s[:], in_=grouped[:].rearrange("p c i -> p (c i)"))

        quantise_w2(0, "w2_first")
        quantise_w2(1, "w2_second")
        for n in range(len(PIECES) - 1):
            gather_words(n, "v_w%d" % n)
        ahead = first_stage(0)
        gather_words(len(PIECES) - 1, "after_first_product")
        for unit in range(len(units)):
            parts = ahead
            if unit + 1 < len(units):
                ahead = first_stage(unit + 1)
            turn_and_put(unit, *parts)
            if unit in (1, 3, 99):
                quantise_w2(len(w2_w), "product%d" % unit)
            if unit == 6:
                quantise_w4("product%d" % unit)

        picked = keep.tile([P, 3, TILES, HALF], F32, name="picked", tag="late")
        for hf in range(2):
            for t in range(TILES):
                nc.vector.tensor_copy(picked[:, hf, t, :], page[t][:].indirect(list3[:, hf * 32 : (hf + 1) * 32]))
        finals = [(hf, t) for hf in range(2) for t in range(TILES)]
        holes = {}

        def gather_holes(n, dst):
            hf, t = finals[n]
            nc.vector.tensor_copy(dst, page[t][:].indirect(list4[:, hf * 32 : (hf + 1) * 32]))
            holes[n] = dst

        for n in range(3):
            gather_holes(n, picked[:, 2, n, :])

        x_w, x_s = [], []
        for hf in range(2):
            for t in range(TILES):
                reread(t, hf)
            grouped = keep.tile([P, HALF, PACK], BF16, name="x_grouped", tag="x_grouped%d" % hf, align_bytes=64)
            words = grouped[:].bitcast(F32)
            for pair in range(CH // 2):
                bank_x = psum.tile([P, 2, 2, P], F32, name="bank_x", tag="bank_x", bufs=2)
                for c in range(2):
                    for u in range(2):
                        nc.tensor.transpose(bank_x[:, c, u, :], x_turned[hf][:, 2 * pair + c, u, :], ident_f[:])
                nc.scalar.copy(
                    words[:, pair * 2 * P : (pair + 1) * 2 * P, :].rearrange("p (c m) u -> p c m u", c=2),
                    bank_x[:].rearrange("p c u m -> p c m u"),
                )
            codes = keep.tile([P, HALF], U32, name="x_w%d" % hf, align_bytes=64)
            scales = keep.tile([P, HALF], U8, name="x_s%d" % hf, align_bytes=64)
            nc.vector.quantize_mx(out=codes[:].bitcast(FP8X4), scales=scales[:], in_=grouped[:].rearrange("p m i -> p (m i)"))
            x_w.append(codes)
            x_s.append(scales)
            if hf == 0:
                held = keep.tile([P, 5 - 3, HALF], F32, name="held", tag="x_grouped0", align_bytes=64)
                for n in range(3, 5):
                    gather_holes(n, held[:, n - 3, :])

        tags = ("bank_a", "bank_b0", "bank_b1", "bank_c")
        waiting = []
        for n, (hf, t) in enumerate(finals):
            if hf == 0:
                y = psum.tile([P, HALF], F32, name="y", tag="bank_x", bufs=2)
            else:
                y = psum.tile([P, HALF], F32, name="y", tag=tags[t])
            nc.tensor.matmul_mx(
                y[:], lhsT=w4_w[:, t * P : (t + 1) * P].bitcast(FP8X4), lhsT_scale=w4_s[:, t * P : (t + 1) * P],
                rhs=x_w[hf][:].bitcast(FP8X4), rhs_scale=x_s[hf][:], start=True, stop=True,
            )
            larger = work.tile([P, HALF], F32, name="larger", bufs=4)
            result = picked[:, hf, t, :]
            rows = out[t * P : (t + 1) * P, hf * HALF : (hf + 1) * HALF]
            if n < 6:
                y_sb = work.tile([P, HALF], F32, name="y_sb", bufs=4)
                nc.scalar.copy(y_sb[:], y[:])
            nc.vector.scalar_tensor_tensor(larger[:], holes[n], water_sb[:, t : t + 1], y[:], ALU.mult, ALU.max)
            if n + 5 < len(finals):
                gather_holes(n + 5, holes[n])
            if n < 6:
                nc.gpsimd.tensor_tensor(result, larger[:], y_sb[:], ALU.add)
                nc.sync.dma_start(rows, result)
            else:
                waiting.append((result, larger, y, rows))
            if len(waiting) == 2 or n == len(finals) - 1:
                for result, larger, y, rows in waiting[: (1 if n < len(finals) - 1 else 2)]:
                    nc.vector.tensor_tensor(result, larger[:], y[:], ALU.add)
                    nc.sync.dma_start(rows, result)
                waiting = waiting[1:]
